import numpy as np
CORES = [125,127,253,255,381,383,509,511]
N = 8
T, CAP = 1024, 256
def entries(a): return a.T.reshape(-1)
def pack(v, P): return np.ascontiguousarray(np.asarray(v, np.int32).reshape(-1, P).T)
def lists(rng, how):
    n = rng.integers(0, CAP + 1, (N, 8))
    if how in ("comb", "full"): n[:] = CAP
    if how == "one": n[:] = 1
    if how == "none": n[int(rng.integers(N))] = 0; n[:, int(rng.integers(8))] = 0
    F = np.zeros((N, 8, T), np.int64)
    for r in range(N):
        for h in range(8):
            o = (rng.permutation(16)[:, None] + 16 * np.arange(T // 16)).reshape(-1) if how == "comb" else rng.permutation(T)
            F[r, h, o[:n[r, h]]] = 1
    if how == "run":
        p = rng.permutation(8); n[:, p[:2]] = CAP; n[:, p[2]] = CAP * rng.permutation(np.arange(N) % 2); n[:, p[3]] = 0
        s = rng.integers(0, T - n + 1); s[:, p[0]] = 0; s[:, p[1]] = T - CAP; s[:, p[2]] = 16 * rng.integers(0, max(1, (T - CAP) // 16), N) + 1
        F = ((np.arange(T) >= s[:, :, None]) & (np.arange(T) < (s + n)[:, :, None])).astype(np.int64)
    return {"keep": np.stack([np.concatenate([pack(F[r, h], 16) for h in range(8)], axis=0) for r in range(N)])}
def setup_inputs(rng):
    return dict({"x": rng.standard_normal((N, 128, T), dtype=np.float32)}, **lists(rng, "uniform"))
def setup_inputs_comb(rng):
    d = setup_inputs(rng); d.update(lists(rng, "comb"))
    for k in ("x",): d[k] = (d[k].astype(np.float32) * 1048576.0).astype(d[k].dtype)
    return d
def setup_inputs_full(rng):
    d = setup_inputs(rng); d.update(lists(rng, "full"))
    for k in ("x",): d[k] = (d[k].astype(np.float32) * (1 / 1024.0)).astype(d[k].dtype)
    return d
def setup_inputs_none(rng):
    d = setup_inputs(rng); d.update(lists(rng, "none"))
    return d
def setup_inputs_one(rng):
    d = setup_inputs(rng); d.update(lists(rng, "one"))
    return d
def setup_inputs_run(rng):
    d = setup_inputs(rng); d.update(lists(rng, "run"))
    return d
def check_inputs(x):
    bad = []
    if x["keep"].min() < 0 or x["keep"].max() >= 2: bad.append("keep out of range")
    if max(int(a[16 * h:16 * h + 16].sum()) for a in x["keep"] for h in range(8)) > CAP: bad.append("a head keeps more than CAP columns on a rank")
    return bad
def reference(x, keep):
    y = np.zeros((128, N * CAP), x.dtype)
    for h in range(8):
        H = slice(16 * h, 16 * h + 16); got = np.concatenate([x[r][H][:, entries(keep[r][H]) > 0] for r in range(N)], axis=1); y[H, :got.shape[1]] = got
    return {"y": np.broadcast_to(y, (N, 128, N * CAP))}

@@ -1,0 +1,271 @@
+from concourse.bass import DstId, RemoteDMATransfer
+from concourse.mybir import AluOpType, ActivationFunctionType
+
+CAP, NR = 256, 8
+HALF = CAP // 2
+ZC = NR * CAP
+PW = 1536
+V_PIECES = [(0, 256), (256, 640), (640, 1024)]
+S_PIECES = [(1024, 1280), (1280, 1664), (1664, 2048)]
+
+SCRATCH = {
+    "kp": ("sbuf", [128, 64], "int32"),
+    "xs": ("sbuf", [128, 1024], "float32"),
+    "pack": ("sbuf", [128, PW], "float32"),
+    "land": ("sbuf", [128, ZC + 16], "float32"),
+    "yb": ("sbuf", [128, ZC], "float32"),
+    "cnt": ("sbuf", [128, 4 * NR], "float32"),
+    "pi": ("sbuf", [128, 1], "int32"), "pmi": ("sbuf", [128, 1], "int32"),
+    "pf": ("sbuf", [128, 1], "float32"), "pm": ("sbuf", [128, 1], "float32"),
+    "p16": ("sbuf", [128, 1], "float32"), "p32": ("sbuf", [128, 1], "float32"),
+    "qf": ("sbuf", [128, 128], "float32"), "jf": ("sbuf", [128, 128], "float32"),
+    "ident": ("sbuf", [128, 128], "float16"), "t1": ("sbuf", [128, 128], "float16"),
+    "t2": ("sbuf", [128, 128], "float16"), "t3": ("sbuf", [128, 128], "float16"),
+    "blk": ("sbuf", [128, 128], "float16"), "low": ("sbuf", [128, 128], "float16"),
+    "jh": ("sbuf", [128, 128], "float16"),
+    "ap": ("sbuf", [128, 64], "float16"), "an": ("sbuf", [128, 64], "float32"),
+    "fh": ("sbuf", [128, 64], "float16"), "nm": ("sbuf", [128, 64], "float16"),
+    "zz": ("sbuf", [128, 64], "float32"),
+    "run": ("sbuf", [128, 64], "float32"), "df": ("sbuf", [128, 64], "float32"),
+    "du": ("sbuf", [128, 64], "uint16"),
+    "ends": ("sbuf", [128, NR], "float32"), "gap": ("sbuf", [128, NR], "float32"),
+    "tm": ("sbuf", [128, 128 * NR], "float16"),
+    "iu": ("sbuf", [128, 128], "uint16"),
+    "psT": ("psum", [128, 512], "float32"),
+    "psD": ("psum", [128, 512], "float32"),
+    "psJ": ("psum", [128, 512], "float32"),
+}
+SEMAPHORES = (["kl", "x0", "x1", "gi", "v", "fh", "nm", "tt", "td", "run", "pk", "own", "oc", "tj", "iu", "st", "sent",
+               "cn", "dat", "p0", "p1", "rc", "q0", "q1"]
+              + ["tm%d" % r for r in range(NR)]
+              + ["yv%d" % k for k in range(len(V_PIECES))] + ["ys%d" % k for k in range(len(S_PIECES))])
+
+
+def bits(m):
+    return [1 << b for b in range(16) if (m >> b) & 1]
+
+
+def plan(T, topo):
+    cores = list(T.cores)
+    by_host = {}
+    for r, c in enumerate(cores):
+        by_host.setdefault(topo.host(c), []).append(r)
+    hosts = sorted(by_host)
+    peer, cable, helpers = {}, {}, {}
+    for h in hosts:
+        c0 = cores[by_host[h][0]]
+        for o in hosts:
+            if o == h or not topo.may_write(c0, cores[by_host[o][0]]):
+                continue
+            if topo.rack(o) == topo.rack(h):
+                peer[h] = o
+            else:
+                cable[h] = o
+        near = [c for c in range(max(cores) + 1)
+                if topo.host(c) == h and topo.chip(c) == topo.chip(c0) and c not in cores]
+        helpers[h] = sorted(near, key=lambda c: (topo.die(c) != topo.die(c0), c))
+    nk = len(by_host[hosts[0]])
+    steps, role = {}, {}
+
+    def masks(src, near, far):
+        off = bits(topo.mask(src, far))
+        on = [b for b in bits(topo.mask(src, near)) if b not in off]
+        return sum(off[0::2]), sum(off[1::2]), sum(on), sum(on[:len(on) // 2]), sum(on[len(on) // 2:])
+
+    for h in hosts:
+        here = [cores[r] for r in by_host[h]]
+        over_p = [cores[r] for r in by_host[peer[h]]]
+        over_c = [cores[r] for r in by_host[cable[h]]]
+        for i in range(nk):
+            r, X = by_host[h][i], here[i]
+            mate, P, K = here[1 - i], over_p[i], helpers[cable[h]][i]
+            even, odd, on, lo, hi = masks(X, mate, P)
+            pr = by_host[peer[h]][i]
+            role[X] = ("rank", r)
+            steps[X] = {
+                "cnt": [("run", r, 0, helpers[peer[h]][nk + i], even, "rc"), ("run", r, 0, K, odd, "rc"),
+                        ("run", r, 0, mate, on, "cn")],
+                "a": [("pack", r, 0, P, even, "p0"), ("pack", r, 1, K, odd, "q1"), ("pack", r, 0, mate, on, "dat")],
+                "b": [("pack", r, 1, P, even, "p1"), ("pack", r, 0, K, odd, "q0"), ("pack", r, 1, mate, on, "dat")],
+                "f0": [("land", pr, 0, over_c[i], even, "dat"), ("land", pr, 0, over_c[1 - i], odd, "dat"),
+                       ("land", pr, 0, mate, on, "dat")],
+                "f1": [("land", pr, 1, mate, on, "dat")],
+            }
+            X, r = helpers[h][i], by_host[cable[h]][i]
+            even, odd, on, lo, hi = masks(X, here[0], over_p[0])
+            role[X] = ("cable", r)
+            steps[X] = {
+                "cnt": [("cnt", r, 0, over_p[i], even, "cn"), ("cnt", r, 0, over_p[1 - i], odd, "cn"),
+                        ("cnt", r, 0, here[i], lo, "cn"), ("cnt", r, 0, here[1 - i], hi, "cn")],
+                "f1": [("land", r, 1, over_p[i], even, "dat"), ("land", r, 1, over_p[1 - i], odd, "dat"),
+                       ("land", r, 1, here[i], lo, "dat"), ("land", r, 1, here[1 - i], hi, "dat")],
+                "f0": [("land", r, 0, here[i], lo, "dat"), ("land", r, 0, here[1 - i], hi, "dat")],
+            }
+            X, r = helpers[h][nk + i], by_host[peer[h]][i]
+            even, odd, on, lo, hi = masks(X, here[0], over_p[0])
+            role[X] = ("peer", r)
+            steps[X] = {"cnt": [("cnt", r, 0, here[i], even + odd, "cn"), ("cnt", r, 0, here[1 - i], on, "cn")]}
+    return steps, role
+
+
+def rank_program(g, core, T, topo):
+    steps, role = plan(T, topo)
+    if core not in role:
+        return
+    S = T.sem
+    due = {}
+    for c in steps:
+        for name in steps[c]:
+            for (what, r, half, dst, mask, sem) in steps[c][name]:
+                if dst == core:
+                    due[sem] = due.get(sem, 0) + len(bits(mask))
+    sent = [0]
+
+    def send(name):
+        tr = []
+        for (what, r, half, dst, mask, sem) in steps[core][name]:
+            a = r * CAP + half * HALF
+            if what == "run":
+                src, out = T.run[:, 63:64], T.cnt[:, 4 * r:4 * r + 1]
+            elif what == "cnt":
+                src, out = T.cnt[:, 4 * r:4 * r + 1], T.cnt[:, 4 * r:4 * r + 1]
+            elif what == "pack":
+                src, out = T.pack[:, half * HALF:(half + 1) * HALF], T.land[:, a:a + HALF]
+            else:
+                src, out = T.land[:, a:a + HALF], T.land[:, a:a + HALF]
+            rid, pid = topo.addr(dst, core)
+            tr.append(RemoteDMATransfer(dst_ids=[DstId(rid=rid, pnc=pid)], dma_engine_mask=mask,
+                                        remote_sem=S[sem], src=src, dst=out))
+            sent[0] += len(bits(mask))
+        g.remote_dma_fused(tr, local_sem=S.sent)
+
+    kind, r = role[core]
+    if kind != "rank":
+        g.wait_ge(S.rc, due["rc"])
+        send("cnt")
+        if kind == "cable":
+            g.wait_ge(S.q1, due["q1"])
+            send("f1")
+            g.wait_ge(S.q0, due["q0"])
+            send("f0")
+        g.wait_ge(S.sent, sent[0])
+        return
+
+    A, COPY = AluOpType, ActivationFunctionType.Copy
+    v, sc, sy, te = g.vector, g.scalar, g.sync, g.tensor
+    nv = [0]
+
+    def inc(ins):
+        ins.then_inc(S.v, 1)
+        nv[0] += 1
+
+    def bar():
+        v.wait_ge(S.v, nv[0])
+
+    sy.dma_start(T.kp[:], T.keep[:]).then_inc(S.kl, 16)
+    sc.dma_start(T.xs[:, 0:512], T.x[:, 0:512]).then_inc(S.x0, 16)
+    sy.dma_start(T.xs[:, 512:1024], T.x[:, 512:1024]).then_inc(S.x1, 16)
+
+    g.iota(T.pi[:], [[0, 1]], 0, 1).then_inc(S.gi, 1)
+    g.iota(T.pf[:], [[0, 1]], 0, 1, allow_small_or_imprecise_dtypes=True).then_inc(S.gi, 1)
+    g.iota(T.qf[:], [[1, 128]], 0, 0, allow_small_or_imprecise_dtypes=True).then_inc(S.gi, 1)
+    g.wait_ge(S.run, 1)
+    send("cnt")
+    g.wait_ge(S.pk, 1)
+    send("a")
+    send("b")
+    g.wait_ge(S.p0, due["p0"])
+    send("f0")
+    g.wait_ge(S.p1, due["p1"])
+    send("f1")
+    g.wait_ge(S.sent, sent[0])
+
+    inc(v.memset(T.pack[:, 0:CAP], 0.0))
+    inc(v.memset(T.land[:, ZC:ZC + 16], 0.0))
+    inc(v.memset(T.zz[:], 0.0))
+    v.wait_ge(S.gi, 3)
+    inc(v.tensor_scalar(T.pmi[:], T.pi[:], 15, None, A.bitwise_and))
+    bar()
+    inc(v.tensor_copy(T.pm[:], T.pmi[:]))
+    bar()
+    inc(v.tensor_scalar(T.p16[:], T.pf[:], T.pm[:], None, A.subtract))
+    inc(v.tensor_scalar(T.p32[:], T.pf[:], T.pm[:], -16.0, A.subtract, A.subtract))
+    inc(v.tensor_scalar(T.jf[:], T.qf[:], 16.0, T.pm[:], A.mult, A.add))
+    inc(v.tensor_scalar(T.ident[:], T.qf[:], T.pf[:], None, A.is_equal))
+    inc(v.tensor_scalar(T.t1[:], T.qf[:], T.pf[:], None, A.is_lt))
+    bar()
+    inc(v.tensor_scalar(T.t2[:], T.qf[:], T.p16[:], None, A.is_lt))
+    inc(v.tensor_scalar(T.t3[:], T.qf[:], T.p32[:], None, A.is_lt))
+    inc(v.tensor_scalar(T.ap[:], T.jf[:, 0:64], 256.0, None, A.add))
+    inc(v.tensor_scalar(T.an[:], T.jf[:, 0:64], -1.0, -257.0, A.mult, A.add))
+    inc(v.tensor_copy(T.jh[:], T.jf[:]))
+    bar()
+    inc(v.tensor_tensor(T.blk[:], T.t3[:], T.t2[:], A.subtract))
+    inc(v.tensor_tensor(T.low[:], T.t2[:], T.t1[:], A.subtract))
+    bar()
+    consts = nv[0]
+
+    v.wait_ge(S.kl, 16)
+    v.tensor_copy(T.fh[:], T.kp[:]).then_inc(S.fh, 1)
+    v.tensor_tensor(T.nm[:], T.kp[:], T.an[:], A.mult).then_inc(S.nm, 1)
+    v.wait_ge(S.tt, 1)
+    v.tensor_tensor_scan(T.run[:], T.psT[:, 0:64], T.zz[:], 0.0, A.add, A.add).then_inc(S.run, 1)
+    v.wait_ge(S.run, 1)
+    v.wait_ge(S.td, 1)
+    inc(v.tensor_tensor(T.df[:], T.psD[:, 0:64], T.run[:], A.add))
+    bar()
+    inc(v.tensor_copy(T.du[:], T.df[:]))
+    bar()
+    v.wait_ge(S.x0, 16)
+    inc(v.tensor_copy(T.pack[:, 0:PW].indirect(T.du[:, 0:32]), T.xs[:, 0:512]))
+    bar()
+    v.wait_ge(S.x1, 16)
+    v.tensor_copy(T.pack[:, 0:PW].indirect(T.du[:, 32:64]), T.xs[:, 512:1024]).then_inc(S.pk, 1)
+
+    te.wait_ge(S.v, consts)
+    te.matmul(T.psD[:, 0:64], T.ident[:], T.ap[:], True, False)
+    te.matmul(T.psJ[:, 0:128], T.ident[:], T.jh[:], True, False)
+    te.wait_ge(S.fh, 1)
+    te.matmul(T.psT[:, 0:64], T.blk[:], T.fh[:], True, True).then_inc(S.tt, 1)
+    te.matmul(T.psD[:, 0:64], T.low[:], T.fh[:], False, False)
+    te.wait_ge(S.nm, 1)
+    te.matmul(T.psD[:, 0:64], T.ident[:], T.nm[:], False, True).then_inc(S.td, 1)
+    for q in range(NR):
+        te.wait_ge(S["tm%d" % q], 1)
+        ins = te.matmul(T.psJ[:, 0:128], T.ident[:], T.tm[:, 128 * q:128 * q + 128], False, q == NR - 1)
+        if q == NR - 1:
+            ins.then_inc(S.tj, 1)
+
+    sc.wait_ge(S.run, 1)
+    sc.activation(T.cnt[:, 4 * r:4 * r + 1], T.run[:, 63:64], COPY).then_inc(S.oc, 1)
+    sc.wait_ge(S.pk, 1)
+    sc.activation(T.land[:, r * CAP:(r + 1) * CAP], T.pack[:, 0:CAP], COPY, bias=-0.0).then_inc(S.own, 1)
+
+    v.wait_ge(S.oc, 1)
+    v.wait_ge(S.cn, due["cn"])
+    inc(v.tensor_tensor_scan(T.ends[:], T.cnt[:, 0:4 * NR:4], T.zz[:, 0:NR], 0.0, A.add, A.add))
+    inc(v.tensor_scalar(T.gap[:], T.cnt[:, 0:4 * NR:4], -1.0, float(CAP), A.mult, A.add))
+    bar()
+    for q in range(NR):
+        v.tensor_scalar(T.tm[:, 128 * q:128 * q + 128], T.jf[:], T.ends[:, q:q + 1], T.gap[:, q:q + 1],
+                        A.is_ge, A.mult).then_inc(S["tm%d" % q], 1)
+    v.wait_ge(S.tj, 1)
+    v.tensor_scalar(T.iu[:], T.psJ[:, 0:128], float(ZC), None, A.min).then_inc(S.iu, 1)
+
+    for q in (v, sc):
+        q.wait_ge(S.iu, 1)
+        q.wait_ge(S.own, 1)
+        for sem in ("p0", "p1", "dat"):
+            q.wait_ge(S[sem], due[sem])
+    for k, (a, b) in enumerate(V_PIECES):
+        v.tensor_copy(T.yb[:, a:b], T.land[:].indirect(T.iu[:, a // 16:b // 16])).then_inc(S["yv%d" % k], 1)
+    for k, (a, b) in enumerate(S_PIECES):
+        sc.activation(T.yb[:, a:b], T.land[:].indirect(T.iu[:, a // 16:b // 16]), COPY,
+                      bias=-0.0).then_inc(S["ys%d" % k], 1)
+    n = 0
+    for k in range(len(V_PIECES)):
+        for name, (a, b) in (("yv%d" % k, V_PIECES[k]), ("ys%d" % k, S_PIECES[k])):
+            sy.wait_ge(S[name], 1)
+            sy.dma_start(T.y[:, a:b], T.yb[:, a:b]).then_inc(S.st, 16)
+            n += 16
+    sy.wait_ge(S.st, n)

@@ -4,9 +4,8 @@ from concourse.mybir import AluOpType, ActivationFunctionType
 CAP, NR = 256, 8
 HALF = CAP // 2
 ZC = NR * CAP
-PW = 1536
-V_PIECES = [(0, 256), (256, 640), (640, 1024)]
-S_PIECES = [(1024, 1280), (1280, 1664), (1664, 2048)]
+PW = 1664
+PIECES = [(0, 256, 512), (512, 896, 1280), (1280, 1664, 2048)]
 
 SCRATCH = {
     "kp": ("sbuf", [128, 64], "int32"),
@@ -15,18 +14,16 @@ SCRATCH = {
     "land": ("sbuf", [128, ZC + 16], "float32"),
     "yb": ("sbuf", [128, ZC], "float32"),
     "cnt": ("sbuf", [128, 4 * NR], "float32"),
-    "pi": ("sbuf", [128, 1], "int32"), "pmi": ("sbuf", [128, 1], "int32"),
-    "pf": ("sbuf", [128, 1], "float32"), "pm": ("sbuf", [128, 1], "float32"),
-    "p16": ("sbuf", [128, 1], "float32"), "p32": ("sbuf", [128, 1], "float32"),
-    "qf": ("sbuf", [128, 128], "float32"), "jf": ("sbuf", [128, 128], "float32"),
-    "ident": ("sbuf", [128, 128], "float16"), "t1": ("sbuf", [128, 128], "float16"),
-    "t2": ("sbuf", [128, 128], "float16"), "t3": ("sbuf", [128, 128], "float16"),
-    "blk": ("sbuf", [128, 128], "float16"), "low": ("sbuf", [128, 128], "float16"),
+    "pi": ("sbuf", [128, 1], "int32"), "pbi": ("sbuf", [128, 1], "int32"), "pmi": ("sbuf", [128, 1], "int32"),
+    "pf": ("sbuf", [128, 1], "float32"), "pb": ("sbuf", [128, 1], "float32"), "pm": ("sbuf", [128, 1], "float32"),
+    "q": ("sbuf", [128, 128], "bfloat16"), "qb": ("sbuf", [128, 128], "bfloat16"),
+    "ident": ("sbuf", [128, 128], "float16"), "blk": ("sbuf", [128, 128], "float16"),
+    "up": ("sbuf", [128, 128], "float16"), "above": ("sbuf", [128, 128], "float16"),
     "jh": ("sbuf", [128, 128], "float16"),
-    "ap": ("sbuf", [128, 64], "float16"), "an": ("sbuf", [128, 64], "float32"),
+    "an": ("sbuf", [128, 64], "float32"), "ap": ("sbuf", [128, 64], "float16"),
     "fh": ("sbuf", [128, 64], "float16"), "nm": ("sbuf", [128, 64], "float16"),
     "zz": ("sbuf", [128, 64], "float32"),
-    "run": ("sbuf", [128, 64], "float32"), "df": ("sbuf", [128, 64], "float32"),
+    "run": ("sbuf", [128, 68], "float32"), "df": ("sbuf", [128, 64], "float32"),
     "du": ("sbuf", [128, 64], "uint16"),
     "ends": ("sbuf", [128, NR], "float32"), "gap": ("sbuf", [128, NR], "float32"),
     "tm": ("sbuf", [128, 128 * NR], "float16"),
@@ -35,10 +32,10 @@ SCRATCH = {
     "psD": ("psum", [128, 512], "float32"),
     "psJ": ("psum", [128, 512], "float32"),
 }
-SEMAPHORES = (["kl", "x0", "x1", "gi", "v", "fh", "nm", "tt", "td", "run", "pk", "own", "oc", "tj", "iu", "st", "sent",
-               "cn", "dat", "p0", "p1", "rc", "q0", "q1"]
+SEMAPHORES = (["kl", "x0", "x1", "g0", "g1", "g2", "g3", "v", "con", "fh", "nm", "tt", "td", "run", "pk", "own", "oc",
+               "jj", "tj", "iu", "st", "sent", "cn", "dat", "p0", "p1", "rc", "q0", "q1"]
               + ["tm%d" % r for r in range(NR)]
-              + ["yv%d" % k for k in range(len(V_PIECES))] + ["ys%d" % k for k in range(len(S_PIECES))])
+              + ["y%d" % k for k in range(len(PIECES))])
 
 
 def bits(m):
@@ -126,7 +123,7 @@ def rank_program(g, core, T, topo):
         for (what, r, half, dst, mask, sem) in steps[core][name]:
             a = r * CAP + half * HALF
             if what == "run":
-                src, out = T.run[:, 63:64], T.cnt[:, 4 * r:4 * r + 1]
+                src, out = T.run[:, 64:65], T.cnt[:, 4 * r:4 * r + 1]
             elif what == "cnt":
                 src, out = T.cnt[:, 4 * r:4 * r + 1], T.cnt[:, 4 * r:4 * r + 1]
             elif what == "pack":
@@ -166,9 +163,10 @@ def rank_program(g, core, T, topo):
     sc.dma_start(T.xs[:, 0:512], T.x[:, 0:512]).then_inc(S.x0, 16)
     sy.dma_start(T.xs[:, 512:1024], T.x[:, 512:1024]).then_inc(S.x1, 16)
 
-    g.iota(T.pi[:], [[0, 1]], 0, 1).then_inc(S.gi, 1)
-    g.iota(T.pf[:], [[0, 1]], 0, 1, allow_small_or_imprecise_dtypes=True).then_inc(S.gi, 1)
-    g.iota(T.qf[:], [[1, 128]], 0, 0, allow_small_or_imprecise_dtypes=True).then_inc(S.gi, 1)
+    g.iota(T.pi[:], [[0, 1]], 0, 1).then_inc(S.g0, 1)
+    g.iota(T.q[:], [[1, 128]], 0, 0, allow_small_or_imprecise_dtypes=True).then_inc(S.g1, 1)
+    g.iota(T.qb[:], [[1, 8], [0, 16]], 0, 0, allow_small_or_imprecise_dtypes=True).then_inc(S.g2, 1)
+    g.iota(T.an[:], [[-16, 64]], -257, -1, allow_small_or_imprecise_dtypes=True).then_inc(S.g3, 1)
     g.wait_ge(S.run, 1)
     send("cnt")
     g.wait_ge(S.pk, 1)
@@ -180,92 +178,89 @@ def rank_program(g, core, T, topo):
     send("f1")
     g.wait_ge(S.sent, sent[0])
 
-    inc(v.memset(T.pack[:, 0:CAP], 0.0))
-    inc(v.memset(T.land[:, ZC:ZC + 16], 0.0))
     inc(v.memset(T.zz[:], 0.0))
-    v.wait_ge(S.gi, 3)
-    inc(v.tensor_scalar(T.pmi[:], T.pi[:], 15, None, A.bitwise_and))
+    inc(v.memset(T.run[:, 0:1], 0.0))
+    v.wait_ge(S.g0, 1)
+    inc(v.tensor_copy(T.pf[:], T.pi[:]))
+    inc(v.tensor_scalar(T.pbi[:], T.pi[:], 4, None, A.arith_shift_right))
     bar()
-    inc(v.tensor_copy(T.pm[:], T.pmi[:]))
+    inc(v.tensor_copy(T.pb[:], T.pbi[:]))
+    inc(v.memset(T.pack[:, 0:CAP], 0.0))
     bar()
-    inc(v.tensor_scalar(T.p16[:], T.pf[:], T.pm[:], None, A.subtract))
-    inc(v.tensor_scalar(T.p32[:], T.pf[:], T.pm[:], -16.0, A.subtract, A.subtract))
-    inc(v.tensor_scalar(T.jf[:], T.qf[:], 16.0, T.pm[:], A.mult, A.add))
-    inc(v.tensor_scalar(T.ident[:], T.qf[:], T.pf[:], None, A.is_equal))
-    inc(v.tensor_scalar(T.t1[:], T.qf[:], T.pf[:], None, A.is_lt))
-    bar()
-    inc(v.tensor_scalar(T.t2[:], T.qf[:], T.p16[:], None, A.is_lt))
-    inc(v.tensor_scalar(T.t3[:], T.qf[:], T.p32[:], None, A.is_lt))
-    inc(v.tensor_scalar(T.ap[:], T.jf[:, 0:64], 256.0, None, A.add))
-    inc(v.tensor_scalar(T.an[:], T.jf[:, 0:64], -1.0, -257.0, A.mult, A.add))
-    inc(v.tensor_copy(T.jh[:], T.jf[:]))
-    bar()
-    inc(v.tensor_tensor(T.blk[:], T.t3[:], T.t2[:], A.subtract))
-    inc(v.tensor_tensor(T.low[:], T.t2[:], T.t1[:], A.subtract))
-    bar()
-    consts = nv[0]
+    v.wait_ge(S.g1, 1)
+    v.tensor_scalar(T.ident[:], T.q[:], T.pf[:], None, A.is_equal).then_inc(S.con, 1)
+    v.tensor_scalar(T.up[:], T.q[:], T.pf[:], None, A.is_ge).then_inc(S.con, 1)
+    v.wait_ge(S.g2, 1)
+    v.tensor_scalar(T.blk[:], T.qb[:], T.pb[:], None, A.is_equal).then_inc(S.con, 1)
+    v.tensor_scalar(T.above[:], T.qb[:], T.pb[:], -1.0, A.is_gt, A.mult).then_inc(S.con, 1)
+    v.wait_ge(S.g3, 1)
+    v.tensor_scalar(T.ap[:], T.an[:], -1.0, -1.0, A.mult, A.add).then_inc(S.con, 1)
 
     v.wait_ge(S.kl, 16)
     v.tensor_copy(T.fh[:], T.kp[:]).then_inc(S.fh, 1)
     v.tensor_tensor(T.nm[:], T.kp[:], T.an[:], A.mult).then_inc(S.nm, 1)
     v.wait_ge(S.tt, 1)
-    v.tensor_tensor_scan(T.run[:], T.psT[:, 0:64], T.zz[:], 0.0, A.add, A.add).then_inc(S.run, 1)
+    v.tensor_tensor_scan(T.run[:, 1:65], T.psT[:, 0:64], T.zz[:], 0.0, A.add, A.add).then_inc(S.run, 1)
     v.wait_ge(S.run, 1)
     v.wait_ge(S.td, 1)
-    inc(v.tensor_tensor(T.df[:], T.psD[:, 0:64], T.run[:], A.add))
+    inc(v.tensor_tensor(T.df[:], T.psD[:, 0:64], T.run[:, 0:64], A.add))
     bar()
     inc(v.tensor_copy(T.du[:], T.df[:]))
     bar()
     v.wait_ge(S.x0, 16)
-    inc(v.tensor_copy(T.pack[:, 0:PW].indirect(T.du[:, 0:32]), T.xs[:, 0:512]))
+    inc(v.tensor_copy(T.pack[:].indirect(T.du[:, 0:32]), T.xs[:, 0:512]))
     bar()
     v.wait_ge(S.x1, 16)
-    v.tensor_copy(T.pack[:, 0:PW].indirect(T.du[:, 32:64]), T.xs[:, 512:1024]).then_inc(S.pk, 1)
+    v.tensor_copy(T.pack[:].indirect(T.du[:, 32:64]), T.xs[:, 512:1024]).then_inc(S.pk, 1)
 
-    te.wait_ge(S.v, consts)
+    te.wait_ge(S.con, 5)
     te.matmul(T.psD[:, 0:64], T.ident[:], T.ap[:], True, False)
-    te.matmul(T.psJ[:, 0:128], T.ident[:], T.jh[:], True, False)
     te.wait_ge(S.fh, 1)
     te.matmul(T.psT[:, 0:64], T.blk[:], T.fh[:], True, True).then_inc(S.tt, 1)
-    te.matmul(T.psD[:, 0:64], T.low[:], T.fh[:], False, False)
+    te.matmul(T.psD[:, 0:64], T.up[:], T.fh[:], False, False)
+    te.matmul(T.psD[:, 0:64], T.above[:], T.fh[:], False, False)
     te.wait_ge(S.nm, 1)
     te.matmul(T.psD[:, 0:64], T.ident[:], T.nm[:], False, True).then_inc(S.td, 1)
-    for q in range(NR):
-        te.wait_ge(S["tm%d" % q], 1)
-        ins = te.matmul(T.psJ[:, 0:128], T.ident[:], T.tm[:, 128 * q:128 * q + 128], False, q == NR - 1)
-        if q == NR - 1:
+    te.wait_ge(S.jj, 1)
+    te.matmul(T.psJ[:, 0:128], T.ident[:], T.jh[:], True, False)
+    for k in range(NR):
+        te.wait_ge(S["tm%d" % k], 1)
+        ins = te.matmul(T.psJ[:, 0:128], T.ident[:], T.tm[:, 128 * k:128 * k + 128], False, k == NR - 1)
+        if k == NR - 1:
             ins.then_inc(S.tj, 1)
 
     sc.wait_ge(S.run, 1)
-    sc.activation(T.cnt[:, 4 * r:4 * r + 1], T.run[:, 63:64], COPY).then_inc(S.oc, 1)
+    sc.activation(T.cnt[:, 4 * r:4 * r + 1], T.run[:, 64:65], COPY).then_inc(S.oc, 1)
     sc.wait_ge(S.pk, 1)
     sc.activation(T.land[:, r * CAP:(r + 1) * CAP], T.pack[:, 0:CAP], COPY, bias=-0.0).then_inc(S.own, 1)
 
+    inc(v.memset(T.land[:, ZC:ZC + 16], 0.0))
+    inc(v.tensor_scalar(T.pmi[:], T.pi[:], 15, None, A.bitwise_and))
+    bar()
+    inc(v.tensor_copy(T.pm[:], T.pmi[:]))
+    bar()
+    v.tensor_scalar(T.jh[:], T.q[:], 16.0, T.pm[:], A.mult, A.add).then_inc(S.jj, 1)
+    v.wait_ge(S.jj, 1)
     v.wait_ge(S.oc, 1)
     v.wait_ge(S.cn, due["cn"])
     inc(v.tensor_tensor_scan(T.ends[:], T.cnt[:, 0:4 * NR:4], T.zz[:, 0:NR], 0.0, A.add, A.add))
     inc(v.tensor_scalar(T.gap[:], T.cnt[:, 0:4 * NR:4], -1.0, float(CAP), A.mult, A.add))
     bar()
-    for q in range(NR):
-        v.tensor_scalar(T.tm[:, 128 * q:128 * q + 128], T.jf[:], T.ends[:, q:q + 1], T.gap[:, q:q + 1],
-                        A.is_ge, A.mult).then_inc(S["tm%d" % q], 1)
+    for k in range(NR):
+        v.tensor_scalar(T.tm[:, 128 * k:128 * k + 128], T.jh[:], T.ends[:, k:k + 1], T.gap[:, k:k + 1],
+                        A.is_ge, A.mult).then_inc(S["tm%d" % k], 1)
     v.wait_ge(S.tj, 1)
     v.tensor_scalar(T.iu[:], T.psJ[:, 0:128], float(ZC), None, A.min).then_inc(S.iu, 1)
 
-    for q in (v, sc):
-        q.wait_ge(S.iu, 1)
-        q.wait_ge(S.own, 1)
+    for queue in (v, sc):
+        queue.wait_ge(S.iu, 1)
+        queue.wait_ge(S.own, 1)
         for sem in ("p0", "p1", "dat"):
-            q.wait_ge(S[sem], due[sem])
-    for k, (a, b) in enumerate(V_PIECES):
-        v.tensor_copy(T.yb[:, a:b], T.land[:].indirect(T.iu[:, a // 16:b // 16])).then_inc(S["yv%d" % k], 1)
-    for k, (a, b) in enumerate(S_PIECES):
-        sc.activation(T.yb[:, a:b], T.land[:].indirect(T.iu[:, a // 16:b // 16]), COPY,
-                      bias=-0.0).then_inc(S["ys%d" % k], 1)
-    n = 0
-    for k in range(len(V_PIECES)):
-        for name, (a, b) in (("yv%d" % k, V_PIECES[k]), ("ys%d" % k, S_PIECES[k])):
-            sy.wait_ge(S[name], 1)
-            sy.dma_start(T.y[:, a:b], T.yb[:, a:b]).then_inc(S.st, 16)
-            n += 16
-    sy.wait_ge(S.st, n)
+            queue.wait_ge(S[sem], due[sem])
+    for k, (a, m, b) in enumerate(PIECES):
+        v.tensor_copy(T.yb[:, a:m], T.land[:].indirect(T.iu[:, a // 16:m // 16])).then_inc(S["y%d" % k], 1)
+        sc.activation(T.yb[:, m:b], T.land[:].indirect(T.iu[:, m // 16:b // 16]), COPY,
+                      bias=-0.0).then_inc(S["y%d" % k], 1)
+        sy.wait_ge(S["y%d" % k], 2)
+        sy.dma_start(T.y[:, a:b], T.yb[:, a:b]).then_inc(S.st, 16)
+    sy.wait_ge(S.st, 16 * len(PIECES))

@@ -2,10 +2,10 @@ from concourse.bass import DstId, RemoteDMATransfer
 from concourse.mybir import AluOpType, ActivationFunctionType
 
 CAP, NR = 256, 8
-HALF = CAP // 2
+QW = 80
 ZC = NR * CAP
 PW = 1664
-PIECES = [(0, 256, 512), (512, 896, 1280), (1280, 1664, 2048)]
+PIECES = [(0, 128, 256), (256, 640, 1024), (1024, 1536, 2048)]
 
 SCRATCH = {
     "kp": ("sbuf", [128, 64], "int32"),
@@ -33,7 +33,7 @@ SCRATCH = {
     "psJ": ("psum", [128, 512], "float32"),
 }
 SEMAPHORES = (["kl", "x0", "x1", "g0", "g1", "g2", "g3", "v", "con", "fh", "nm", "tt", "td", "run", "pk", "own", "oc",
-               "jj", "tj", "iu", "st", "sent", "cn", "dat", "p0", "p1", "rc", "q0", "q1"]
+               "jj", "tj", "iu", "st", "sent", "cn", "dat", "fromp", "fromc", "rc", "rd"]
               + ["tm%d" % r for r in range(NR)]
               + ["y%d" % k for k in range(len(PIECES))])
 
@@ -48,7 +48,7 @@ def plan(T, topo):
     for r, c in enumerate(cores):
         by_host.setdefault(topo.host(c), []).append(r)
     hosts = sorted(by_host)
-    peer, cable, helpers = {}, {}, {}
+    peer, cable, via_p, via_c = {}, {}, {}, {}
     for h in hosts:
         c0 = cores[by_host[h][0]]
         for o in hosts:
@@ -58,50 +58,52 @@ def plan(T, topo):
                 peer[h] = o
             else:
                 cable[h] = o
-        near = [c for c in range(max(cores) + 1)
+        free = [c for c in range(max(cores) + 1)
                 if topo.host(c) == h and topo.chip(c) == topo.chip(c0) and c not in cores]
-        helpers[h] = sorted(near, key=lambda c: (topo.die(c) != topo.die(c0), c))
-    nk = len(by_host[hosts[0]])
+        own_die = [c for c in free if topo.die(c) == topo.die(c0)]
+        far_die = [c for c in free if topo.die(c) != topo.die(c0)]
+        via_p[h] = far_die[0::2]
+        via_c[h] = [own_die[0], far_die[1]]
     steps, role = {}, {}
+    Q, R = (0, QW), (QW, CAP)
 
     def masks(src, near, far):
         off = bits(topo.mask(src, far))
         on = [b for b in bits(topo.mask(src, near)) if b not in off]
-        return sum(off[0::2]), sum(off[1::2]), sum(on), sum(on[:len(on) // 2]), sum(on[len(on) // 2:])
+        return sum(off[0::2]), sum(off[1::2]), on
 
     for h in hosts:
         here = [cores[r] for r in by_host[h]]
         over_p = [cores[r] for r in by_host[peer[h]]]
         over_c = [cores[r] for r in by_host[cable[h]]]
-        for i in range(nk):
+        for i in range(len(here)):
             r, X = by_host[h][i], here[i]
-            mate, P, K = here[1 - i], over_p[i], helpers[cable[h]][i]
-            even, odd, on, lo, hi = masks(X, mate, P)
-            pr = by_host[peer[h]][i]
+            mate, KP, KC = here[1 - i], via_p[peer[h]][i], via_c[cable[h]][i]
+            even, odd, on = masks(X, mate, over_p[i])
+            on = sum(on)
             role[X] = ("rank", r)
             steps[X] = {
-                "cnt": [("run", r, 0, helpers[peer[h]][nk + i], even, "rc"), ("run", r, 0, K, odd, "rc"),
-                        ("run", r, 0, mate, on, "cn")],
-                "a": [("pack", r, 0, P, even, "p0"), ("pack", r, 1, K, odd, "q1"), ("pack", r, 0, mate, on, "dat")],
-                "b": [("pack", r, 1, P, even, "p1"), ("pack", r, 0, K, odd, "q0"), ("pack", r, 1, mate, on, "dat")],
-                "f0": [("land", pr, 0, over_c[i], even, "dat"), ("land", pr, 0, over_c[1 - i], odd, "dat"),
-                       ("land", pr, 0, mate, on, "dat")],
-                "f1": [("land", pr, 1, mate, on, "dat")],
+                "cnt": [("run", r, Q, KP, even, "rc"), ("run", r, Q, KC, odd, "rc"), ("run", r, Q, mate, on, "cn")],
+                "a": [("pack", r, R, KC, odd, "rd"), ("pack", r, R, mate, on, "dat")],
+                "b": [("pack", r, Q, KP, even, "rd"), ("pack", r, Q, over_c[i], odd, "fromc"),
+                      ("pack", r, Q, mate, on, "dat")],
+                "c": [("pack", r, R, over_p[i], even, "fromp")],
+                "fp": [("land", by_host[peer[h]][i], R, mate, on, "dat")],
+                "fc": [("land", by_host[cable[h]][i], Q, mate, on, "dat")],
             }
-            X, r = helpers[h][i], by_host[cable[h]][i]
-            even, odd, on, lo, hi = masks(X, here[0], over_p[0])
-            role[X] = ("cable", r)
-            steps[X] = {
-                "cnt": [("cnt", r, 0, over_p[i], even, "cn"), ("cnt", r, 0, over_p[1 - i], odd, "cn"),
-                        ("cnt", r, 0, here[i], lo, "cn"), ("cnt", r, 0, here[1 - i], hi, "cn")],
-                "f1": [("land", r, 1, over_p[i], even, "dat"), ("land", r, 1, over_p[1 - i], odd, "dat"),
-                       ("land", r, 1, here[i], lo, "dat"), ("land", r, 1, here[1 - i], hi, "dat")],
-                "f0": [("land", r, 0, here[i], lo, "dat"), ("land", r, 0, here[1 - i], hi, "dat")],
-            }
-            X, r = helpers[h][nk + i], by_host[peer[h]][i]
-            even, odd, on, lo, hi = masks(X, here[0], over_p[0])
-            role[X] = ("peer", r)
-            steps[X] = {"cnt": [("cnt", r, 0, here[i], even + odd, "cn"), ("cnt", r, 0, here[1 - i], on, "cn")]}
+            for X, r, part, beyond in ((via_p[h][i], by_host[peer[h]][i], Q, over_c),
+                                       (via_c[h][i], by_host[cable[h]][i], R, over_p)):
+                even, odd, on = masks(X, here[0], beyond[0])
+                lo, hi = sum(on[:len(on) // 2]), sum(on[len(on) // 2:])
+                role[X] = ("helper", r)
+                inside = [(here[i], lo), (here[1 - i], hi)]
+                outside = [(beyond[i], even), (beyond[1 - i], odd)]
+                steps[X] = {"f": [("land", r, part, d, m, "dat") for d, m in outside + inside]}
+                if beyond is over_p:
+                    steps[X]["cnt"] = [("cnt", r, part, d, m, "cn") for d, m in outside + inside]
+                else:
+                    steps[X]["cnt"] = [("cnt", r, part, here[i], even + odd, "cn"),
+                                       ("cnt", r, part, here[1 - i], lo + hi, "cn")]
     return steps, role
 
 
@@ -113,23 +115,23 @@ def rank_program(g, core, T, topo):
     due = {}
     for c in steps:
         for name in steps[c]:
-            for (what, r, half, dst, mask, sem) in steps[c][name]:
+            for (what, r, cols, dst, mask, sem) in steps[c][name]:
                 if dst == core:
                     due[sem] = due.get(sem, 0) + len(bits(mask))
     sent = [0]
 
     def send(name):
         tr = []
-        for (what, r, half, dst, mask, sem) in steps[core][name]:
-            a = r * CAP + half * HALF
+        for (what, r, cols, dst, mask, sem) in steps[core][name]:
+            a, b = r * CAP + cols[0], r * CAP + cols[1]
             if what == "run":
                 src, out = T.run[:, 64:65], T.cnt[:, 4 * r:4 * r + 1]
             elif what == "cnt":
                 src, out = T.cnt[:, 4 * r:4 * r + 1], T.cnt[:, 4 * r:4 * r + 1]
             elif what == "pack":
-                src, out = T.pack[:, half * HALF:(half + 1) * HALF], T.land[:, a:a + HALF]
+                src, out = T.pack[:, cols[0]:cols[1]], T.land[:, a:b]
             else:
-                src, out = T.land[:, a:a + HALF], T.land[:, a:a + HALF]
+                src, out = T.land[:, a:b], T.land[:, a:b]
             rid, pid = topo.addr(dst, core)
             tr.append(RemoteDMATransfer(dst_ids=[DstId(rid=rid, pnc=pid)], dma_engine_mask=mask,
                                         remote_sem=S[sem], src=src, dst=out))
@@ -137,14 +139,11 @@ def rank_program(g, core, T, topo):
         g.remote_dma_fused(tr, local_sem=S.sent)
 
     kind, r = role[core]
-    if kind != "rank":
+    if kind == "helper":
         g.wait_ge(S.rc, due["rc"])
         send("cnt")
-        if kind == "cable":
-            g.wait_ge(S.q1, due["q1"])
-            send("f1")
-            g.wait_ge(S.q0, due["q0"])
-            send("f0")
+        g.wait_ge(S.rd, due["rd"])
+        send("f")
         g.wait_ge(S.sent, sent[0])
         return
 
@@ -172,10 +171,11 @@ def rank_program(g, core, T, topo):
     g.wait_ge(S.pk, 1)
     send("a")
     send("b")
-    g.wait_ge(S.p0, due["p0"])
-    send("f0")
-    g.wait_ge(S.p1, due["p1"])
-    send("f1")
+    send("c")
+    g.wait_ge(S.fromp, due["fromp"])
+    send("fp")
+    g.wait_ge(S.fromc, due["fromc"])
+    send("fc")
     g.wait_ge(S.sent, sent[0])
 
     inc(v.memset(T.zz[:], 0.0))
@@ -255,7 +255,7 @@ def rank_program(g, core, T, topo):
     for queue in (v, sc):
         queue.wait_ge(S.iu, 1)
         queue.wait_ge(S.own, 1)
-        for sem in ("p0", "p1", "dat"):
+        for sem in ("fromp", "fromc", "dat"):
             queue.wait_ge(S[sem], due[sem])
     for k, (a, m, b) in enumerate(PIECES):
         v.tensor_copy(T.yb[:, a:m], T.land[:].indirect(T.iu[:, a // 16:m // 16])).then_inc(S["y%d" % k], 1)

@@ -2,9 +2,9 @@ from concourse.bass import DstId, RemoteDMATransfer
 from concourse.mybir import AluOpType, ActivationFunctionType
 
 CAP, NR = 256, 8
-QW = 80
+R1W, RW = 96, 176
 ZC = NR * CAP
-PW = 1664
+PW = 2784
 PIECES = [(0, 128, 256), (256, 640, 1024), (1024, 1536, 2048)]
 
 SCRATCH = {
@@ -16,24 +16,26 @@ SCRATCH = {
     "cnt": ("sbuf", [128, 4 * NR], "float32"),
     "pi": ("sbuf", [128, 1], "int32"), "pbi": ("sbuf", [128, 1], "int32"), "pmi": ("sbuf", [128, 1], "int32"),
     "pf": ("sbuf", [128, 1], "float32"), "pb": ("sbuf", [128, 1], "float32"), "pm": ("sbuf", [128, 1], "float32"),
-    "q": ("sbuf", [128, 128], "bfloat16"), "qb": ("sbuf", [128, 128], "bfloat16"),
-    "ident": ("sbuf", [128, 128], "float16"), "blk": ("sbuf", [128, 128], "float16"),
-    "up": ("sbuf", [128, 128], "float16"), "above": ("sbuf", [128, 128], "float16"),
+    "sub": ("sbuf", [128, 1], "float32"),
+    "ones": ("sbuf", [128, 128], "bfloat16"), "q": ("sbuf", [128, 128], "bfloat16"),
+    "qb": ("sbuf", [128, 128], "bfloat16"),
+    "ident": ("sbuf", [128, 128], "float16"), "blk": ("sbuf", [128, 128], "bfloat16"),
+    "up": ("sbuf", [128, 128], "bfloat16"), "above": ("sbuf", [128, 128], "bfloat16"),
     "jh": ("sbuf", [128, 128], "float16"),
-    "an": ("sbuf", [128, 64], "float32"), "ap": ("sbuf", [128, 64], "float16"),
-    "fh": ("sbuf", [128, 64], "float16"), "nm": ("sbuf", [128, 64], "float16"),
-    "zz": ("sbuf", [128, 64], "float32"),
-    "run": ("sbuf", [128, 68], "float32"), "df": ("sbuf", [128, 64], "float32"),
+    "tt": ("sbuf", [128, 64], "float32"), "t2": ("sbuf", [128, 64], "float16"),
+    "kf": ("sbuf", [128, 64], "bfloat16"), "z": ("sbuf", [128, 64], "float16"),
+    "run": ("sbuf", [128, 68], "bfloat16"),
     "du": ("sbuf", [128, 64], "uint16"),
-    "ends": ("sbuf", [128, NR], "float32"), "gap": ("sbuf", [128, NR], "float32"),
+    "full": ("sbuf", [128, NR], "float32"), "ends": ("sbuf", [128, NR], "float32"), "gap": ("sbuf", [128, NR], "float32"),
     "tm": ("sbuf", [128, 128 * NR], "float16"),
     "iu": ("sbuf", [128, 128], "uint16"),
-    "psT": ("psum", [128, 512], "float32"),
+    "psC": ("psum", [128, 512], "float32"),
     "psD": ("psum", [128, 512], "float32"),
+    "psZ": ("psum", [128, 512], "float32"),
     "psJ": ("psum", [128, 512], "float32"),
 }
-SEMAPHORES = (["kl", "x0", "x1", "g0", "g1", "g2", "g3", "v", "con", "fh", "nm", "tt", "td", "run", "pk", "own", "oc",
-               "jj", "tj", "iu", "st", "sent", "cn", "dat", "fromp", "fromc", "rc", "rd"]
+SEMAPHORES = (["kl", "x0", "x1", "g0", "g1", "g2", "gf", "r0", "pt", "v", "q", "pb", "sub", "pz", "con", "kf", "z", "td", "c",
+               "run", "pk", "own", "oc", "jj", "tj", "iu", "st", "sent", "cn", "dat", "fromp", "fromc", "rc", "rd"]
               + ["tm%d" % r for r in range(NR)]
               + ["y%d" % k for k in range(len(PIECES))])
 
@@ -63,14 +65,14 @@ def plan(T, topo):
         own_die = [c for c in free if topo.die(c) == topo.die(c0)]
         far_die = [c for c in free if topo.die(c) != topo.die(c0)]
         via_p[h] = far_die[0::2]
-        via_c[h] = [own_die[0], far_die[1]]
+        via_c[h] = [far_die[1::2], own_die]
     steps, role = {}, {}
-    Q, R = (0, QW), (QW, CAP)
+    R1, R2, R, Q, BLOCK = (0, R1W), (R1W, RW), (0, RW), (RW, CAP), (0, CAP)
 
     def masks(src, near, far):
         off = bits(topo.mask(src, far))
         on = [b for b in bits(topo.mask(src, near)) if b not in off]
-        return sum(off[0::2]), sum(off[1::2]), on
+        return off[0::2], off[1::2], on
 
     for h in hosts:
         here = [cores[r] for r in by_host[h]]
@@ -78,32 +80,34 @@ def plan(T, topo):
         over_c = [cores[r] for r in by_host[cable[h]]]
         for i in range(len(here)):
             r, X = by_host[h][i], here[i]
-            mate, KP, KC = here[1 - i], via_p[peer[h]][i], via_c[cable[h]][i]
+            mate, KP = here[1 - i], via_p[peer[h]][i]
+            KC1, KC2 = via_c[cable[h]][0][i], via_c[cable[h]][1][i]
             even, odd, on = masks(X, mate, over_p[i])
-            on = sum(on)
+            odd1, odd2 = sum(odd[0::2]), sum(odd[1::2])
+            even, odd, on = sum(even), sum(odd), sum(on)
+            every = topo.mask(X, mate)
             role[X] = ("rank", r)
             steps[X] = {
-                "cnt": [("run", r, Q, KP, even, "rc"), ("run", r, Q, KC, odd, "rc"), ("run", r, Q, mate, on, "cn")],
-                "a": [("pack", r, R, KC, odd, "rd"), ("pack", r, R, mate, on, "dat")],
-                "b": [("pack", r, Q, KP, even, "rd"), ("pack", r, Q, over_c[i], odd, "fromc"),
-                      ("pack", r, Q, mate, on, "dat")],
+                "cnt": [("cnt", r, Q, KP, even, "rc"), ("cnt", r, Q, KC1, odd1, "rc"), ("cnt", r, Q, KC2, odd2, "rc"),
+                        ("cnt", r, Q, mate, on, "cn")],
+                "a": [("pack", r, R1, KC1, odd, "rd")],
+                "b": [("pack", r, R2, KC2, odd, "rd"), ("pack", r, Q, KP, even, "rd")],
                 "c": [("pack", r, R, over_p[i], even, "fromp")],
-                "fp": [("land", by_host[peer[h]][i], R, mate, on, "dat")],
-                "fc": [("land", by_host[cable[h]][i], Q, mate, on, "dat")],
+                "d": [("pack", r, Q, over_c[i], odd, "fromc")],
+                "e": [("pack", r, BLOCK, mate, on, "dat")],
+                "fp": [("land", by_host[peer[h]][i], R, mate, every, "dat")],
+                "fc": [("land", by_host[cable[h]][i], Q, mate, every, "dat")],
             }
-            for X, r, part, beyond in ((via_p[h][i], by_host[peer[h]][i], Q, over_c),
-                                       (via_c[h][i], by_host[cable[h]][i], R, over_p)):
+            for X, r, part, beyond, k in ((via_p[h][i], by_host[peer[h]][i], Q, over_c, None),
+                                          (via_c[h][0][i], by_host[cable[h]][i], R1, over_p, i),
+                                          (via_c[h][1][i], by_host[cable[h]][i], R2, over_p, 1 - i)):
                 even, odd, on = masks(X, here[0], beyond[0])
-                lo, hi = sum(on[:len(on) // 2]), sum(on[len(on) // 2:])
+                even, odd, lo, hi = sum(even), sum(odd), sum(on[:len(on) // 2]), sum(on[len(on) // 2:])
                 role[X] = ("helper", r)
-                inside = [(here[i], lo), (here[1 - i], hi)]
-                outside = [(beyond[i], even), (beyond[1 - i], odd)]
-                steps[X] = {"f": [("land", r, part, d, m, "dat") for d, m in outside + inside]}
-                if beyond is over_p:
-                    steps[X]["cnt"] = [("cnt", r, part, d, m, "cn") for d, m in outside + inside]
-                else:
-                    steps[X]["cnt"] = [("cnt", r, part, here[i], even + odd, "cn"),
-                                       ("cnt", r, part, here[1 - i], lo + hi, "cn")]
+                first, second = (here[i], here[1 - i]) if k is None else (beyond[k], here[k])
+                steps[X] = {"cnt": [("cnt", r, part, first, even + odd, "cn"), ("cnt", r, part, second, lo + hi, "cn")],
+                            "off": [("land", r, part, beyond[i], even, "dat"), ("land", r, part, beyond[1 - i], odd, "dat")],
+                            "on": [("land", r, part, here[i], lo, "dat"), ("land", r, part, here[1 - i], hi, "dat")]}
     return steps, role
 
 
@@ -124,9 +128,7 @@ def rank_program(g, core, T, topo):
         tr = []
         for (what, r, cols, dst, mask, sem) in steps[core][name]:
             a, b = r * CAP + cols[0], r * CAP + cols[1]
-            if what == "run":
-                src, out = T.run[:, 64:65], T.cnt[:, 4 * r:4 * r + 1]
-            elif what == "cnt":
+            if what == "cnt":
                 src, out = T.cnt[:, 4 * r:4 * r + 1], T.cnt[:, 4 * r:4 * r + 1]
             elif what == "pack":
                 src, out = T.pack[:, cols[0]:cols[1]], T.land[:, a:b]
@@ -143,7 +145,8 @@ def rank_program(g, core, T, topo):
         g.wait_ge(S.rc, due["rc"])
         send("cnt")
         g.wait_ge(S.rd, due["rd"])
-        send("f")
+        send("off")
+        send("on")
         g.wait_ge(S.sent, sent[0])
         return
 
@@ -159,68 +162,69 @@ def rank_program(g, core, T, topo):
         v.wait_ge(S.v, nv[0])
 
     sy.dma_start(T.kp[:], T.keep[:]).then_inc(S.kl, 16)
-    sc.dma_start(T.xs[:, 0:512], T.x[:, 0:512]).then_inc(S.x0, 16)
-    sy.dma_start(T.xs[:, 512:1024], T.x[:, 512:1024]).then_inc(S.x1, 16)
+    sy.dma_start(T.xs[:, 0:512], T.x[:, 0:512]).then_inc(S.x0, 16)
 
     g.iota(T.pi[:], [[0, 1]], 0, 1).then_inc(S.g0, 1)
-    g.iota(T.q[:], [[1, 128]], 0, 0, allow_small_or_imprecise_dtypes=True).then_inc(S.g1, 1)
-    g.iota(T.qb[:], [[1, 8], [0, 16]], 0, 0, allow_small_or_imprecise_dtypes=True).then_inc(S.g2, 1)
-    g.iota(T.an[:], [[-16, 64]], -257, -1, allow_small_or_imprecise_dtypes=True).then_inc(S.g3, 1)
-    g.wait_ge(S.run, 1)
+    g.iota(T.pf[:], [[0, 1]], 0, 1, allow_small_or_imprecise_dtypes=True).then_inc(S.gf, 1)
+    g.iota(T.qb[:], [[1, 8], [0, 16]], 0, 0, allow_small_or_imprecise_dtypes=True).then_inc(S.g1, 1)
+    g.iota(T.tt[:], [[-32, 64]], -258, -2, allow_small_or_imprecise_dtypes=True).then_inc(S.g2, 1)
+    g.wait_ge(S.oc, 1)
     send("cnt")
     g.wait_ge(S.pk, 1)
-    send("a")
-    send("b")
-    send("c")
+    for name in ("a", "b", "c", "d", "e"):
+        send(name)
     g.wait_ge(S.fromp, due["fromp"])
     send("fp")
     g.wait_ge(S.fromc, due["fromc"])
     send("fc")
     g.wait_ge(S.sent, sent[0])
 
-    inc(v.memset(T.zz[:], 0.0))
-    inc(v.memset(T.run[:, 0:1], 0.0))
+    inc(v.memset(T.ones[:], 1.0))
+    bar()
+    v.tensor_tensor_scan(T.q[:], T.ones[:], T.ones[:], -1.0, A.add, A.mult).then_inc(S.q, 1)
     v.wait_ge(S.g0, 1)
-    inc(v.tensor_copy(T.pf[:], T.pi[:]))
     inc(v.tensor_scalar(T.pbi[:], T.pi[:], 4, None, A.arith_shift_right))
     bar()
-    inc(v.tensor_copy(T.pb[:], T.pbi[:]))
-    inc(v.memset(T.pack[:, 0:CAP], 0.0))
-    bar()
-    v.wait_ge(S.g1, 1)
+    v.tensor_copy(T.pb[:], T.pbi[:]).then_inc(S.pb, 1)
+    v.wait_ge(S.q, 1)
+    v.wait_ge(S.gf, 1)
     v.tensor_scalar(T.ident[:], T.q[:], T.pf[:], None, A.is_equal).then_inc(S.con, 1)
-    v.tensor_scalar(T.up[:], T.q[:], T.pf[:], None, A.is_ge).then_inc(S.con, 1)
+    v.tensor_scalar(T.up[:], T.q[:], T.pf[:], -1.0, A.is_ge, A.mult).then_inc(S.con, 1)
+    v.wait_ge(S.pb, 1)
+    v.wait_ge(S.g1, 1)
+    v.tensor_scalar(T.blk[:], T.qb[:], T.pb[:], -1.0, A.is_equal, A.mult).then_inc(S.con, 1)
+    v.tensor_scalar(T.above[:], T.qb[:], T.pb[:], None, A.is_gt).then_inc(S.con, 1)
     v.wait_ge(S.g2, 1)
-    v.tensor_scalar(T.blk[:], T.qb[:], T.pb[:], None, A.is_equal).then_inc(S.con, 1)
-    v.tensor_scalar(T.above[:], T.qb[:], T.pb[:], -1.0, A.is_gt, A.mult).then_inc(S.con, 1)
-    v.wait_ge(S.g3, 1)
-    v.tensor_scalar(T.ap[:], T.an[:], -1.0, -1.0, A.mult, A.add).then_inc(S.con, 1)
+    v.tensor_scalar(T.t2[:], T.tt[:], -2.0, None, A.mult).then_inc(S.con, 1)
 
+    v.wait_ge(S.pt, 1)
     v.wait_ge(S.kl, 16)
-    v.tensor_copy(T.fh[:], T.kp[:]).then_inc(S.fh, 1)
-    v.tensor_tensor(T.nm[:], T.kp[:], T.an[:], A.mult).then_inc(S.nm, 1)
-    v.wait_ge(S.tt, 1)
-    v.tensor_tensor_scan(T.run[:, 1:65], T.psT[:, 0:64], T.zz[:], 0.0, A.add, A.add).then_inc(S.run, 1)
-    v.wait_ge(S.run, 1)
+    v.tensor_scalar(T.kf[:], T.kp[:], -1.0, 2.0, A.mult, A.add).then_inc(S.kf, 1)
+    v.tensor_tensor(T.z[:], T.kp[:], T.psZ[:, 0:64], A.mult).then_inc(S.z, 1)
+    v.wait_ge(S.kf, 1)
+    v.tensor_tensor_scan(T.run[:, 1:65], T.kf[:], T.ones[:, 0:64], 0.0, A.add, A.mult).then_inc(S.run, 1)
+    v.wait_ge(S.sub, 1)
     v.wait_ge(S.td, 1)
-    inc(v.tensor_tensor(T.df[:], T.psD[:, 0:64], T.run[:, 0:64], A.add))
-    bar()
-    inc(v.tensor_copy(T.du[:], T.df[:]))
-    bar()
+    inc(v.tensor_scalar(T.du[:], T.psD[:, 0:64], T.sub[:], None, A.subtract))
+    v.wait_ge(S.pz, 2)
     v.wait_ge(S.x0, 16)
-    inc(v.tensor_copy(T.pack[:].indirect(T.du[:, 0:32]), T.xs[:, 0:512]))
     bar()
+    inc(v.tensor_copy(T.pack[:].indirect(T.du[:, 0:32]), T.xs[:, 0:512]))
     v.wait_ge(S.x1, 16)
+    bar()
     v.tensor_copy(T.pack[:].indirect(T.du[:, 32:64]), T.xs[:, 512:1024]).then_inc(S.pk, 1)
 
     te.wait_ge(S.con, 5)
-    te.matmul(T.psD[:, 0:64], T.ident[:], T.ap[:], True, False)
-    te.wait_ge(S.fh, 1)
-    te.matmul(T.psT[:, 0:64], T.blk[:], T.fh[:], True, True).then_inc(S.tt, 1)
-    te.matmul(T.psD[:, 0:64], T.up[:], T.fh[:], False, False)
-    te.matmul(T.psD[:, 0:64], T.above[:], T.fh[:], False, False)
-    te.wait_ge(S.nm, 1)
-    te.matmul(T.psD[:, 0:64], T.ident[:], T.nm[:], False, True).then_inc(S.td, 1)
+    te.matmul(T.psD[:, 0:64], T.ident[:], T.t2[:], True, False)
+    te.wait_ge(S.kf, 1)
+    te.matmul(T.psD[:, 0:64], T.up[:], T.kf[:], False, False)
+    te.matmul(T.psD[:, 0:64], T.above[:], T.kf[:], False, False)
+    te.wait_ge(S.z, 1)
+    te.matmul(T.psD[:, 0:64], T.ident[:], T.z[:], False, False)
+    te.wait_ge(S.r0, 1)
+    te.wait_ge(S.run, 1)
+    te.matmul(T.psD[:, 0:64], T.blk[:], T.run[:, 0:64], False, True).then_inc(S.td, 1)
+    te.matmul(T.psC[:, 0:1], T.blk[:], T.run[:, 64:65], True, True).then_inc(S.c, 1)
     te.wait_ge(S.jj, 1)
     te.matmul(T.psJ[:, 0:128], T.ident[:], T.jh[:], True, False)
     for k in range(NR):
@@ -229,12 +233,22 @@ def rank_program(g, core, T, topo):
         if k == NR - 1:
             ins.then_inc(S.tj, 1)
 
-    sc.wait_ge(S.run, 1)
-    sc.activation(T.cnt[:, 4 * r:4 * r + 1], T.run[:, 64:65], COPY).then_inc(S.oc, 1)
+    sc.wait_ge(S.q, 1)
+    sc.dma_start(T.xs[:, 512:1024], T.x[:, 512:1024]).then_inc(S.x1, 16)
+    sc.activation(T.run[:, 0:1], T.q[:, 0:1], COPY, scale=0.0).then_inc(S.r0, 1)
+    sc.wait_ge(S.pb, 1)
+    sc.activation(T.sub[:], T.pb[:], COPY, bias=257.0, scale=32.0).then_inc(S.sub, 1)
+    sc.wait_ge(S.g2, 1)
+    sc.activation(T.psZ[:, 0:64], T.tt[:], COPY).then_inc(S.pt, 1)
+    sc.activation(T.pack[:, 0:128], T.q[:], COPY, scale=0.0).then_inc(S.pz, 1)
+    sc.activation(T.pack[:, 128:256], T.q[:], COPY, scale=0.0).then_inc(S.pz, 1)
+    sc.wait_ge(S.c, 1)
+    sc.activation(T.cnt[:, 4 * r:4 * r + 1], T.psC[:, 0:1], COPY).then_inc(S.oc, 1)
     sc.wait_ge(S.pk, 1)
     sc.activation(T.land[:, r * CAP:(r + 1) * CAP], T.pack[:, 0:CAP], COPY, bias=-0.0).then_inc(S.own, 1)
 
     inc(v.memset(T.land[:, ZC:ZC + 16], 0.0))
+    inc(v.memset(T.full[:], 2048.0))
     inc(v.tensor_scalar(T.pmi[:], T.pi[:], 15, None, A.bitwise_and))
     bar()
     inc(v.tensor_copy(T.pm[:], T.pmi[:]))
@@ -243,8 +257,8 @@ def rank_program(g, core, T, topo):
     v.wait_ge(S.jj, 1)
     v.wait_ge(S.oc, 1)
     v.wait_ge(S.cn, due["cn"])
-    inc(v.tensor_tensor_scan(T.ends[:], T.cnt[:, 0:4 * NR:4], T.zz[:, 0:NR], 0.0, A.add, A.add))
-    inc(v.tensor_scalar(T.gap[:], T.cnt[:, 0:4 * NR:4], -1.0, float(CAP), A.mult, A.add))
+    inc(v.tensor_tensor_scan(T.ends[:], T.cnt[:, 0:4 * NR:4], T.full[:], 0.0, A.add, A.add))
+    inc(v.tensor_scalar(T.gap[:], T.cnt[:, 0:4 * NR:4], -1.0, CAP - 2048.0, A.mult, A.add))
     bar()
     for k in range(NR):
         v.tensor_scalar(T.tm[:, 128 * k:128 * k + 128], T.jh[:], T.ends[:, k:k + 1], T.gap[:, k:k + 1],

from concourse.bass import DstId, RemoteDMATransfer
from concourse.mybir import AluOpType, ActivationFunctionType

CAP, NR = 256, 8
R1W, RW = 96, 176
ZC = NR * CAP
PW = 2784
PIECES = [(0, 128, 256), (256, 640, 1024), (1024, 1536, 2048)]

SCRATCH = {
    "kp": ("sbuf", [128, 64], "int32"),
    "xs": ("sbuf", [128, 1024], "float32"),
    "pack": ("sbuf", [128, PW], "float32"),
    "land": ("sbuf", [128, ZC + 16], "float32"),
    "yb": ("sbuf", [128, ZC], "float32"),
    "cnt": ("sbuf", [128, 4 * NR], "float32"),
    "pi": ("sbuf", [128, 1], "int32"), "pbi": ("sbuf", [128, 1], "int32"), "pmi": ("sbuf", [128, 1], "int32"),
    "pf": ("sbuf", [128, 1], "float32"), "pb": ("sbuf", [128, 1], "float32"), "pm": ("sbuf", [128, 1], "float32"),
    "sub": ("sbuf", [128, 1], "float32"),
    "ones": ("sbuf", [128, 128], "bfloat16"), "q": ("sbuf", [128, 128], "bfloat16"),
    "qb": ("sbuf", [128, 128], "bfloat16"),
    "ident": ("sbuf", [128, 128], "float16"), "blk": ("sbuf", [128, 128], "bfloat16"),
    "up": ("sbuf", [128, 128], "bfloat16"), "above": ("sbuf", [128, 128], "bfloat16"),
    "jh": ("sbuf", [128, 128], "float16"),
    "tt": ("sbuf", [128, 64], "float32"), "t2": ("sbuf", [128, 64], "float16"),
    "kf": ("sbuf", [128, 64], "bfloat16"), "z": ("sbuf", [128, 64], "float16"),
    "run": ("sbuf", [128, 68], "bfloat16"),
    "du": ("sbuf", [128, 64], "uint16"),
    "full": ("sbuf", [128, NR], "float32"), "ends": ("sbuf", [128, NR], "float32"), "gap": ("sbuf", [128, NR], "float32"),
    "tm": ("sbuf", [128, 128 * NR], "float16"),
    "iu": ("sbuf", [128, 128], "uint16"),
    "psC": ("psum", [128, 512], "float32"),
    "psD": ("psum", [128, 512], "float32"),
    "psZ": ("psum", [128, 512], "float32"),
    "psJ": ("psum", [128, 512], "float32"),
}
SEMAPHORES = (["kl", "x0", "x1", "g0", "g1", "g2", "gf", "r0", "pt", "v", "q", "pb", "sub", "pz", "con", "kf", "z", "td", "c",
               "run", "pk", "own", "oc", "jj", "tj", "iu", "st", "sent", "cn", "dat", "fromp", "fromc", "rc", "rd"]
              + ["tm%d" % r for r in range(NR)]
              + ["y%d" % k for k in range(len(PIECES))])


def bits(m):
    return [1 << b for b in range(16) if (m >> b) & 1]


def plan(T, topo):
    cores = list(T.cores)
    by_host = {}
    for r, c in enumerate(cores):
        by_host.setdefault(topo.host(c), []).append(r)
    hosts = sorted(by_host)
    peer, cable, via_p, via_c = {}, {}, {}, {}
    for h in hosts:
        c0 = cores[by_host[h][0]]
        for o in hosts:
            if o == h or not topo.may_write(c0, cores[by_host[o][0]]):
                continue
            if topo.rack(o) == topo.rack(h):
                peer[h] = o
            else:
                cable[h] = o
        free = [c for c in range(max(cores) + 1)
                if topo.host(c) == h and topo.chip(c) == topo.chip(c0) and c not in cores]
        own_die = [c for c in free if topo.die(c) == topo.die(c0)]
        far_die = [c for c in free if topo.die(c) != topo.die(c0)]
        via_p[h] = far_die[0::2]
        via_c[h] = [far_die[1::2], own_die]
    steps, role = {}, {}
    R1, R2, R, Q, BLOCK = (0, R1W), (R1W, RW), (0, RW), (RW, CAP), (0, CAP)

    def masks(src, near, far):
        off = bits(topo.mask(src, far))
        on = [b for b in bits(topo.mask(src, near)) if b not in off]
        return off[0::2], off[1::2], on

    for h in hosts:
        here = [cores[r] for r in by_host[h]]
        over_p = [cores[r] for r in by_host[peer[h]]]
        over_c = [cores[r] for r in by_host[cable[h]]]
        for i in range(len(here)):
            r, X = by_host[h][i], here[i]
            mate, KP = here[1 - i], via_p[peer[h]][i]
            KC1, KC2 = via_c[cable[h]][0][i], via_c[cable[h]][1][i]
            even, odd, on = masks(X, mate, over_p[i])
            odd1, odd2 = sum(odd[0::2]), sum(odd[1::2])
            even, odd, on = sum(even), sum(odd), sum(on)
            every = topo.mask(X, mate)
            role[X] = ("rank", r)
            steps[X] = {
                "cnt": [("cnt", r, Q, KP, even, "rc"), ("cnt", r, Q, KC1, odd1, "rc"), ("cnt", r, Q, KC2, odd2, "rc"),
                        ("cnt", r, Q, mate, on, "cn")],
                "a": [("pack", r, R1, KC1, odd, "rd")],
                "b": [("pack", r, R2, KC2, odd, "rd"), ("pack", r, Q, KP, even, "rd")],
                "c": [("pack", r, R, over_p[i], even, "fromp")],
                "d": [("pack", r, Q, over_c[i], odd, "fromc")],
                "e": [("pack", r, BLOCK, mate, on, "dat")],
                "fp": [("land", by_host[peer[h]][i], R, mate, every, "dat")],
                "fc": [("land", by_host[cable[h]][i], Q, mate, every, "dat")],
            }
            for X, r, part, beyond, k in ((via_p[h][i], by_host[peer[h]][i], Q, over_c, None),
                                          (via_c[h][0][i], by_host[cable[h]][i], R1, over_p, i),
                                          (via_c[h][1][i], by_host[cable[h]][i], R2, over_p, 1 - i)):
                even, odd, on = masks(X, here[0], beyond[0])
                even, odd, lo, hi = sum(even), sum(odd), sum(on[:len(on) // 2]), sum(on[len(on) // 2:])
                role[X] = ("helper", r)
                first, second = (here[i], here[1 - i]) if k is None else (beyond[k], here[k])
                steps[X] = {"cnt": [("cnt", r, part, first, even + odd, "cn"), ("cnt", r, part, second, lo + hi, "cn")],
                            "off": [("land", r, part, beyond[i], even, "dat"), ("land", r, part, beyond[1 - i], odd, "dat")],
                            "on": [("land", r, part, here[i], lo, "dat"), ("land", r, part, here[1 - i], hi, "dat")]}
    return steps, role


def rank_program(g, core, T, topo):
    steps, role = plan(T, topo)
    if core not in role:
        return
    S = T.sem
    due = {}
    for c in steps:
        for name in steps[c]:
            for (what, r, cols, dst, mask, sem) in steps[c][name]:
                if dst == core:
                    due[sem] = due.get(sem, 0) + len(bits(mask))
    sent = [0]

    def send(name):
        tr = []
        for (what, r, cols, dst, mask, sem) in steps[core][name]:
            a, b = r * CAP + cols[0], r * CAP + cols[1]
            if what == "cnt":
                src, out = T.cnt[:, 4 * r:4 * r + 1], T.cnt[:, 4 * r:4 * r + 1]
            elif what == "pack":
                src, out = T.pack[:, cols[0]:cols[1]], T.land[:, a:b]
            else:
                src, out = T.land[:, a:b], T.land[:, a:b]
            rid, pid = topo.addr(dst, core)
            tr.append(RemoteDMATransfer(dst_ids=[DstId(rid=rid, pnc=pid)], dma_engine_mask=mask,
                                        remote_sem=S[sem], src=src, dst=out))
            sent[0] += len(bits(mask))
        g.remote_dma_fused(tr, local_sem=S.sent)

    kind, r = role[core]
    if kind == "helper":
        g.wait_ge(S.rc, due["rc"])
        send("cnt")
        g.wait_ge(S.rd, due["rd"])
        send("off")
        send("on")
        g.wait_ge(S.sent, sent[0])
        return

    A, COPY = AluOpType, ActivationFunctionType.Copy
    v, sc, sy, te = g.vector, g.scalar, g.sync, g.tensor
    nv = [0]

    def inc(ins):
        ins.then_inc(S.v, 1)
        nv[0] += 1

    def bar():
        v.wait_ge(S.v, nv[0])

    sy.dma_start(T.kp[:], T.keep[:]).then_inc(S.kl, 16)
    sy.dma_start(T.xs[:, 0:512], T.x[:, 0:512]).then_inc(S.x0, 16)

    g.iota(T.pi[:], [[0, 1]], 0, 1).then_inc(S.g0, 1)
    g.iota(T.pf[:], [[0, 1]], 0, 1, allow_small_or_imprecise_dtypes=True).then_inc(S.gf, 1)
    g.iota(T.qb[:], [[1, 8], [0, 16]], 0, 0, allow_small_or_imprecise_dtypes=True).then_inc(S.g1, 1)
    g.iota(T.tt[:], [[-32, 64]], -258, -2, allow_small_or_imprecise_dtypes=True).then_inc(S.g2, 1)
    g.wait_ge(S.oc, 1)
    send("cnt")
    g.wait_ge(S.pk, 1)
    for name in ("a", "b", "c", "d", "e"):
        send(name)
    g.wait_ge(S.fromp, due["fromp"])
    send("fp")
    g.wait_ge(S.fromc, due["fromc"])
    send("fc")
    g.wait_ge(S.sent, sent[0])

    inc(v.memset(T.ones[:], 1.0))
    bar()
    v.tensor_tensor_scan(T.q[:], T.ones[:], T.ones[:], -1.0, A.add, A.mult).then_inc(S.q, 1)
    v.wait_ge(S.g0, 1)
    inc(v.tensor_scalar(T.pbi[:], T.pi[:], 4, None, A.arith_shift_right))
    bar()
    v.tensor_copy(T.pb[:], T.pbi[:]).then_inc(S.pb, 1)
    v.wait_ge(S.q, 1)
    v.wait_ge(S.gf, 1)
    v.tensor_scalar(T.ident[:], T.q[:], T.pf[:], None, A.is_equal).then_inc(S.con, 1)
    v.tensor_scalar(T.up[:], T.q[:], T.pf[:], -1.0, A.is_ge, A.mult).then_inc(S.con, 1)
    v.wait_ge(S.pb, 1)
    v.wait_ge(S.g1, 1)
    v.tensor_scalar(T.blk[:], T.qb[:], T.pb[:], -1.0, A.is_equal, A.mult).then_inc(S.con, 1)
    v.tensor_scalar(T.above[:], T.qb[:], T.pb[:], None, A.is_gt).then_inc(S.con, 1)
    v.wait_ge(S.g2, 1)
    v.tensor_scalar(T.t2[:], T.tt[:], -2.0, None, A.mult).then_inc(S.con, 1)

    v.wait_ge(S.pt, 1)
    v.wait_ge(S.kl, 16)
    v.tensor_scalar(T.kf[:], T.kp[:], -1.0, 2.0, A.mult, A.add).then_inc(S.kf, 1)
    v.tensor_tensor(T.z[:], T.kp[:], T.psZ[:, 0:64], A.mult).then_inc(S.z, 1)
    v.wait_ge(S.kf, 1)
    v.tensor_tensor_scan(T.run[:, 1:65], T.kf[:], T.ones[:, 0:64], 0.0, A.add, A.mult).then_inc(S.run, 1)
    v.wait_ge(S.sub, 1)
    v.wait_ge(S.td, 1)
    inc(v.tensor_scalar(T.du[:], T.psD[:, 0:64], T.sub[:], None, A.subtract))
    v.wait_ge(S.pz, 2)
    v.wait_ge(S.x0, 16)
    bar()
    inc(v.tensor_copy(T.pack[:].indirect(T.du[:, 0:32]), T.xs[:, 0:512]))
    v.wait_ge(S.x1, 16)
    bar()
    v.tensor_copy(T.pack[:].indirect(T.du[:, 32:64]), T.xs[:, 512:1024]).then_inc(S.pk, 1)

    te.wait_ge(S.con, 5)
    te.matmul(T.psD[:, 0:64], T.ident[:], T.t2[:], True, False)
    te.wait_ge(S.kf, 1)
    te.matmul(T.psD[:, 0:64], T.up[:], T.kf[:], False, False)
    te.matmul(T.psD[:, 0:64], T.above[:], T.kf[:], False, False)
    te.wait_ge(S.z, 1)
    te.matmul(T.psD[:, 0:64], T.ident[:], T.z[:], False, False)
    te.wait_ge(S.r0, 1)
    te.wait_ge(S.run, 1)
    te.matmul(T.psD[:, 0:64], T.blk[:], T.run[:, 0:64], False, True).then_inc(S.td, 1)
    te.matmul(T.psC[:, 0:1], T.blk[:], T.run[:, 64:65], True, True).then_inc(S.c, 1)
    te.wait_ge(S.jj, 1)
    te.matmul(T.psJ[:, 0:128], T.ident[:], T.jh[:], True, False)
    for k in range(NR):
        te.wait_ge(S["tm%d" % k], 1)
        ins = te.matmul(T.psJ[:, 0:128], T.ident[:], T.tm[:, 128 * k:128 * k + 128], False, k == NR - 1)
        if k == NR - 1:
            ins.then_inc(S.tj, 1)

    sc.wait_ge(S.q, 1)
    sc.dma_start(T.xs[:, 512:1024], T.x[:, 512:1024]).then_inc(S.x1, 16)
    sc.activation(T.run[:, 0:1], T.q[:, 0:1], COPY, scale=0.0).then_inc(S.r0, 1)
    sc.wait_ge(S.pb, 1)
    sc.activation(T.sub[:], T.pb[:], COPY, bias=257.0, scale=32.0).then_inc(S.sub, 1)
    sc.wait_ge(S.g2, 1)
    sc.activation(T.psZ[:, 0:64], T.tt[:], COPY).then_inc(S.pt, 1)
    sc.activation(T.pack[:, 0:128], T.q[:], COPY, scale=0.0).then_inc(S.pz, 1)
    sc.activation(T.pack[:, 128:256], T.q[:], COPY, scale=0.0).then_inc(S.pz, 1)
    sc.wait_ge(S.c, 1)
    sc.activation(T.cnt[:, 4 * r:4 * r + 1], T.psC[:, 0:1], COPY).then_inc(S.oc, 1)
    sc.wait_ge(S.pk, 1)
    sc.activation(T.land[:, r * CAP:(r + 1) * CAP], T.pack[:, 0:CAP], COPY, bias=-0.0).then_inc(S.own, 1)

    inc(v.memset(T.land[:, ZC:ZC + 16], 0.0))
    inc(v.memset(T.full[:], 2048.0))
    inc(v.tensor_scalar(T.pmi[:], T.pi[:], 15, None, A.bitwise_and))
    bar()
    inc(v.tensor_copy(T.pm[:], T.pmi[:]))
    bar()
    v.tensor_scalar(T.jh[:], T.q[:], 16.0, T.pm[:], A.mult, A.add).then_inc(S.jj, 1)
    v.wait_ge(S.jj, 1)
    v.wait_ge(S.oc, 1)
    v.wait_ge(S.cn, due["cn"])
    inc(v.tensor_tensor_scan(T.ends[:], T.cnt[:, 0:4 * NR:4], T.full[:], 0.0, A.add, A.add))
    inc(v.tensor_scalar(T.gap[:], T.cnt[:, 0:4 * NR:4], -1.0, CAP - 2048.0, A.mult, A.add))
    bar()
    for k in range(NR):
        v.tensor_scalar(T.tm[:, 128 * k:128 * k + 128], T.jh[:], T.ends[:, k:k + 1], T.gap[:, k:k + 1],
                        A.is_ge, A.mult).then_inc(S["tm%d" % k], 1)
    v.wait_ge(S.tj, 1)
    v.tensor_scalar(T.iu[:], T.psJ[:, 0:128], float(ZC), None, A.min).then_inc(S.iu, 1)

    for queue in (v, sc):
        queue.wait_ge(S.iu, 1)
        queue.wait_ge(S.own, 1)
        for sem in ("fromp", "fromc", "dat"):
            queue.wait_ge(S[sem], due[sem])
    for k, (a, m, b) in enumerate(PIECES):
        v.tensor_copy(T.yb[:, a:m], T.land[:].indirect(T.iu[:, a // 16:m // 16])).then_inc(S["y%d" % k], 1)
        sc.activation(T.yb[:, m:b], T.land[:].indirect(T.iu[:, m // 16:b // 16]), COPY,
                      bias=-0.0).then_inc(S["y%d" % k], 1)
        sy.wait_ge(S["y%d" % k], 2)
        sy.dma_start(T.y[:, a:b], T.yb[:, a:b]).then_inc(S.st, 16)
    sy.wait_ge(S.st, 16 * len(PIECES))
